import numpy as np, ml_dtypes
CORES = [1,7,41,47,81,87,121,127]
N = 8
G1 = [7,6,5,4,3,2,1,0]
G2 = [0,2,4,6]
G3 = [1,3,5,7]
ROOT3 = 0
def setup_inputs(rng):
    return {"x1": rng.standard_normal((N, 128, 32), dtype=np.float32), "x2": rng.standard_normal((N, 128, 16), dtype=np.float32), "x3": rng.standard_normal((N, 128, 2), dtype=np.float32).astype(ml_dtypes.bfloat16)}
def reference(x1, x2, x3):
    out = {}
    y = np.full((N, 128, 32), np.nan, x1.dtype)
    for i, r in enumerate(G1):
        y[G1[(i + 1) % 8]] = x1[r]
    out["y1"] = y
    y = np.full((N, 128, 4), np.nan, x2.dtype)
    s = x2[G2].sum(axis=0, dtype=np.float64).astype(x2.dtype)
    for i, r in enumerate(G2):
        y[r] = s[:, 4 * i:4 * i + 4]
    out["y2"] = y
    y = np.full((N, 128, 8), np.nan, x3.dtype)
    y[G3[ROOT3]] = np.concatenate([x3[r] for r in G3], axis=1)
    out["y3"] = y
    return out

@@ -1,0 +1,120 @@
+from concourse.bass import DstId, RemoteDMATransfer
+from concourse.mybir import AluOpType
+
+SCRATCH = {
+    "a1": ("dram", [2, 128, 16], "float32"),
+    "b1": ("dram", [2, 128, 16], "float32"),
+    "c1": ("dram", [2, 128, 16], "float32"),
+    "e1": ("dram", [128, 32], "float32"),
+    "f1": ("dram", [128, 32], "float32"),
+    "a2": ("dram", [128, 16], "float32"),
+    "p2": ("dram", [128, 16], "float32"),
+    "q2": ("dram", [2, 128, 16], "float32"),
+    "r2": ("dram", [128, 16], "float32"),
+    "a3": ("dram", [128, 2], "bfloat16"),
+    "l3": ("sbuf", [128, 8], "bfloat16"),
+}
+SEMAPHORES = ["ld", "ld3", "x1in", "x2in", "f2in", "g3in", "acc", "st", "st3", "sent"]
+
+
+def rank_program(g, core, T, topo):
+    S = T.sem
+    chip = topo.chip
+    cores = list(T.cores)
+    G1, G2, G3 = T.tables["G1"], T.tables["G2"], T.tables["G3"]
+    m2 = [cores[r] for r in G2]
+    m3 = [cores[r] for r in G3]
+    root3 = m3[T.tables["ROOT3"]]
+    nxt = {cores[G1[i]]: cores[G1[(i + 1) % len(G1)]] for i in range(len(G1))}
+
+    def did(c):
+        rid, pid, _ = topo.addr(c)
+        return DstId(rid=rid, pnc=pid)
+
+    def par(c):
+        return chip(c) & 1
+
+    def relay1(d):
+        return (chip(d) ^ 1) * 8 + 6
+
+    def relay2(d):
+        return (chip(d) ^ 1) * 8 + 2
+
+    for s, d in nxt.items():
+        if chip(s) != chip(d) and core == relay1(d):
+            g.wait_ge(S.x1in, 4)
+            g.remote_dma_fused(
+                [RemoteDMATransfer(dst_ids=[did(d)], dma_engine_mask=0x0F << (4 * h), remote_sem=S.x1in,
+                                   src=T.b1[h], dst=T.c1[h]) for h in (0, 1)],
+                local_sem=S.sent)
+            g.wait_ge(S.sent, 8)
+            return
+    for d in m2:
+        if core == relay2(d):
+            g.wait_ge(S.x2in, 8)
+            g.remote_dma_fused(
+                [RemoteDMATransfer(dst_ids=[did(d)], dma_engine_mask=0xFF, remote_sem=S.f2in,
+                                   srcs=[T.q2[0], T.q2[1]], dsts=[T.r2[:]], alu_op=1)],
+                local_sem=S.sent)
+            g.wait_ge(S.sent, 8)
+            return
+
+    if T.rank_of(core) is None:
+        return
+
+    if core in m2:
+        j = m2.index(core)
+        cols = slice(4 * j, 4 * j + 4)
+        slot = [m for m in m2 if par(m) == par(core)].index(core)
+        g.sync.dma_start(T.a1[:], T.x1[:]).then_inc(S.ld, 16)
+        g.scalar.dma_start(T.a2[:], T.x2[:]).then_inc(S.ld, 16)
+        g.scalar.dma_start(T.y2[:], T.x2[:, cols]).then_inc(S.x2in, 16)
+
+        r1 = relay1(nxt[core])
+        far = [m for m in m2 if par(m) != par(core)]
+        near = [m for m in m2 if par(m) == par(core) and m != core]
+        g.wait_ge(S.ld, 32)
+        g.remote_dma_fused(
+            [RemoteDMATransfer(dst_ids=[did(r1)], dma_engine_mask=0x03 << (2 * h), remote_sem=S.x1in,
+                               src=T.a1[h], dst=T.b1[h]) for h in (0, 1)]
+            + [RemoteDMATransfer(dst_ids=[did(relay2(m)) for m in far] + [did(m) for m in near],
+                                 dma_engine_mask=0xF0, remote_sem=S.x2in, srcs=[T.a2[:]],
+                                 dsts=[T.q2[slot] for m in far] + [T.p2[:] for m in near])],
+            local_sem=S.sent)
+
+        g.sync.wait_ge(S.x1in, 16)
+        g.sync.dma_start(T.y1[:], T.f1[:]).then_inc(S.st, 16)
+        g.sync.wait_ge(S.st, 16)
+
+        g.wait_ge(S.x2in, 16 + 4 * len(near))
+        g.dma_start(T.y2[:], T.p2[:, cols], accum_op=AluOpType.add).then_inc(S.acc, 16)
+        g.wait_ge(S.acc, 16)
+        g.wait_ge(S.f2in, 8)
+        g.dma_start(T.y2[:], T.r2[:, cols], accum_op=AluOpType.add).then_inc(S.acc, 16)
+        g.wait_ge(S.acc, 32)
+        g.wait_ge(S.sent, 8)
+        return
+
+    k = m3.index(core)
+    sent = 0
+    g.sync.dma_start(T.e1[:], T.x1[:]).then_inc(S.ld, 16)
+    if core != root3:
+        g.scalar.dma_start(T.a3[:], T.x3[:]).then_inc(S.ld3, 16)
+        rid, pid, _ = topo.addr(root3)
+        g.wait_ge(S.ld3, 16)
+        g.remote_dma(T.l3[:, 2 * k:2 * k + 2], T.a3[:], S.g3in, S.sent, pid, rid, 0xFF)
+        sent += 8
+    else:
+        g.scalar.dma_start(T.l3[:, 2 * k:2 * k + 2], T.x3[:]).then_inc(S.g3in, 16)
+        g.scalar.wait_ge(S.g3in, 16 + 8 * (len(m3) - 1))
+        g.scalar.dma_start(T.y3[:], T.l3[:]).then_inc(S.st3, 16)
+        g.scalar.wait_ge(S.st3, 16)
+    rid, pid, _ = topo.addr(nxt[core])
+    g.wait_ge(S.ld, 16)
+    g.remote_dma(T.f1[:], T.e1[:], S.x1in, S.sent, pid, rid, 0xFFFF)
+    sent += 16
+
+    g.sync.wait_ge(S.x1in, 8)
+    g.sync.dma_start(T.y1[:], T.c1[:]).then_inc(S.st, 16)
+    g.sync.wait_ge(S.st, 16)
+    g.wait_ge(S.sent, sent)

@@ -34,15 +34,15 @@ def rank_program(g, core, T, topo):
     def par(c):
         return chip(c) & 1
 
-    def relay1(d):
-        return (chip(d) ^ 1) * 8 + 6
+    def relay1(s):
+        return chip(s) * 8 + 6
 
     def relay2(d):
         return (chip(d) ^ 1) * 8 + 2
 
     for s, d in nxt.items():
-        if chip(s) != chip(d) and core == relay1(d):
-            g.wait_ge(S.x1in, 4)
+        if chip(s) != chip(d) and core == relay1(s):
+            g.wait_ge(S.x1in, 8)
             g.remote_dma_fused(
                 [RemoteDMATransfer(dst_ids=[did(d)], dma_engine_mask=0x0F << (4 * h), remote_sem=S.x1in,
                                    src=T.b1[h], dst=T.c1[h]) for h in (0, 1)],
@@ -51,7 +51,7 @@ def rank_program(g, core, T, topo):
             return
     for d in m2:
         if core == relay2(d):
-            g.wait_ge(S.x2in, 8)
+            g.wait_ge(S.x2in, 16)
             g.remote_dma_fused(
                 [RemoteDMATransfer(dst_ids=[did(d)], dma_engine_mask=0xFF, remote_sem=S.f2in,
                                    srcs=[T.q2[0], T.q2[1]], dsts=[T.r2[:]], alu_op=1)],
@@ -70,15 +70,15 @@ def rank_program(g, core, T, topo):
         g.scalar.dma_start(T.a2[:], T.x2[:]).then_inc(S.ld, 16)
         g.scalar.dma_start(T.y2[:], T.x2[:, cols]).then_inc(S.x2in, 16)
 
-        r1 = relay1(nxt[core])
+        r1 = relay1(core)
         far = [m for m in m2 if par(m) != par(core)]
         near = [m for m in m2 if par(m) == par(core) and m != core]
         g.wait_ge(S.ld, 32)
         g.remote_dma_fused(
-            [RemoteDMATransfer(dst_ids=[did(r1)], dma_engine_mask=0x03 << (2 * h), remote_sem=S.x1in,
+            [RemoteDMATransfer(dst_ids=[did(r1)], dma_engine_mask=0x0F00 << (4 * h), remote_sem=S.x1in,
                                src=T.a1[h], dst=T.b1[h]) for h in (0, 1)]
             + [RemoteDMATransfer(dst_ids=[did(relay2(m)) for m in far] + [did(m) for m in near],
-                                 dma_engine_mask=0xF0, remote_sem=S.x2in, srcs=[T.a2[:]],
+                                 dma_engine_mask=0xFF, remote_sem=S.x2in, srcs=[T.a2[:]],
                                  dsts=[T.q2[slot] for m in far] + [T.p2[:] for m in near])],
             local_sem=S.sent)
 
@@ -86,13 +86,13 @@ def rank_program(g, core, T, topo):
         g.sync.dma_start(T.y1[:], T.f1[:]).then_inc(S.st, 16)
         g.sync.wait_ge(S.st, 16)
 
-        g.wait_ge(S.x2in, 16 + 4 * len(near))
+        g.wait_ge(S.x2in, 16 + 8 * len(near))
         g.dma_start(T.y2[:], T.p2[:, cols], accum_op=AluOpType.add).then_inc(S.acc, 16)
         g.wait_ge(S.acc, 16)
         g.wait_ge(S.f2in, 8)
         g.dma_start(T.y2[:], T.r2[:, cols], accum_op=AluOpType.add).then_inc(S.acc, 16)
         g.wait_ge(S.acc, 32)
-        g.wait_ge(S.sent, 8)
+        g.wait_ge(S.sent, 16)
         return
 
     k = m3.index(core)

from concourse.bass import DstId, RemoteDMATransfer
from concourse.mybir import AluOpType

SCRATCH = {
    "a1": ("dram", [2, 128, 16], "float32"),
    "b1": ("dram", [2, 128, 16], "float32"),
    "c1": ("dram", [2, 128, 16], "float32"),
    "e1": ("dram", [128, 32], "float32"),
    "f1": ("dram", [128, 32], "float32"),
    "a2": ("dram", [128, 16], "float32"),
    "p2": ("dram", [128, 16], "float32"),
    "q2": ("dram", [2, 128, 16], "float32"),
    "r2": ("dram", [128, 16], "float32"),
    "a3": ("dram", [128, 2], "bfloat16"),
    "l3": ("sbuf", [128, 8], "bfloat16"),
}
SEMAPHORES = ["ld", "ld3", "x1in", "x2in", "f2in", "g3in", "acc", "st", "st3", "sent"]


def rank_program(g, core, T, topo):
    S = T.sem
    chip = topo.chip
    cores = list(T.cores)
    G1, G2, G3 = T.tables["G1"], T.tables["G2"], T.tables["G3"]
    m2 = [cores[r] for r in G2]
    m3 = [cores[r] for r in G3]
    root3 = m3[T.tables["ROOT3"]]
    nxt = {cores[G1[i]]: cores[G1[(i + 1) % len(G1)]] for i in range(len(G1))}

    def did(c):
        rid, pid, _ = topo.addr(c)
        return DstId(rid=rid, pnc=pid)

    def par(c):
        return chip(c) & 1

    def relay1(s):
        return chip(s) * 8 + 6

    def relay2(d):
        return (chip(d) ^ 1) * 8 + 2

    for s, d in nxt.items():
        if chip(s) != chip(d) and core == relay1(s):
            g.wait_ge(S.x1in, 8)
            g.remote_dma_fused(
                [RemoteDMATransfer(dst_ids=[did(d)], dma_engine_mask=0x0F << (4 * h), remote_sem=S.x1in,
                                   src=T.b1[h], dst=T.c1[h]) for h in (0, 1)],
                local_sem=S.sent)
            g.wait_ge(S.sent, 8)
            return
    for d in m2:
        if core == relay2(d):
            g.wait_ge(S.x2in, 16)
            g.remote_dma_fused(
                [RemoteDMATransfer(dst_ids=[did(d)], dma_engine_mask=0xFF, remote_sem=S.f2in,
                                   srcs=[T.q2[0], T.q2[1]], dsts=[T.r2[:]], alu_op=1)],
                local_sem=S.sent)
            g.wait_ge(S.sent, 8)
            return

    if T.rank_of(core) is None:
        return

    if core in m2:
        j = m2.index(core)
        cols = slice(4 * j, 4 * j + 4)
        slot = [m for m in m2 if par(m) == par(core)].index(core)
        g.sync.dma_start(T.a1[:], T.x1[:]).then_inc(S.ld, 16)
        g.scalar.dma_start(T.a2[:], T.x2[:]).then_inc(S.ld, 16)
        g.scalar.dma_start(T.y2[:], T.x2[:, cols]).then_inc(S.x2in, 16)

        r1 = relay1(core)
        far = [m for m in m2 if par(m) != par(core)]
        near = [m for m in m2 if par(m) == par(core) and m != core]
        g.wait_ge(S.ld, 32)
        g.remote_dma_fused(
            [RemoteDMATransfer(dst_ids=[did(r1)], dma_engine_mask=0x0F00 << (4 * h), remote_sem=S.x1in,
                               src=T.a1[h], dst=T.b1[h]) for h in (0, 1)]
            + [RemoteDMATransfer(dst_ids=[did(relay2(m)) for m in far] + [did(m) for m in near],
                                 dma_engine_mask=0xFF, remote_sem=S.x2in, srcs=[T.a2[:]],
                                 dsts=[T.q2[slot] for m in far] + [T.p2[:] for m in near])],
            local_sem=S.sent)

        g.sync.wait_ge(S.x1in, 16)
        g.sync.dma_start(T.y1[:], T.f1[:]).then_inc(S.st, 16)
        g.sync.wait_ge(S.st, 16)

        g.wait_ge(S.x2in, 16 + 8 * len(near))
        g.dma_start(T.y2[:], T.p2[:, cols], accum_op=AluOpType.add).then_inc(S.acc, 16)
        g.wait_ge(S.acc, 16)
        g.wait_ge(S.f2in, 8)
        g.dma_start(T.y2[:], T.r2[:, cols], accum_op=AluOpType.add).then_inc(S.acc, 16)
        g.wait_ge(S.acc, 32)
        g.wait_ge(S.sent, 16)
        return

    k = m3.index(core)
    sent = 0
    g.sync.dma_start(T.e1[:], T.x1[:]).then_inc(S.ld, 16)
    if core != root3:
        g.scalar.dma_start(T.a3[:], T.x3[:]).then_inc(S.ld3, 16)
        rid, pid, _ = topo.addr(root3)
        g.wait_ge(S.ld3, 16)
        g.remote_dma(T.l3[:, 2 * k:2 * k + 2], T.a3[:], S.g3in, S.sent, pid, rid, 0xFF)
        sent += 8
    else:
        g.scalar.dma_start(T.l3[:, 2 * k:2 * k + 2], T.x3[:]).then_inc(S.g3in, 16)
        g.scalar.wait_ge(S.g3in, 16 + 8 * (len(m3) - 1))
        g.scalar.dma_start(T.y3[:], T.l3[:]).then_inc(S.st3, 16)
        g.scalar.wait_ge(S.st3, 16)
    rid, pid, _ = topo.addr(nxt[core])
    g.wait_ge(S.ld, 16)
    g.remote_dma(T.f1[:], T.e1[:], S.x1in, S.sent, pid, rid, 0xFFFF)
    sent += 16

    g.sync.wait_ge(S.x1in, 8)
    g.sync.dma_start(T.y1[:], T.c1[:]).then_inc(S.st, 16)
    g.sync.wait_ge(S.st, 16)
    g.wait_ge(S.sent, sent)
